import numpy as np, ml_dtypes
CORES = [0,1,2,3]
N = 4
ROUNDS = 6
def setup_inputs(rng):
    return {"x": rng.standard_normal((N, ROUNDS, 128, 64), dtype=np.float32).astype(ml_dtypes.bfloat16)}
def reference(x):
    g = np.concatenate(list(x), axis=2)
    return {"y": np.broadcast_to(g, (N,) + g.shape)}

import concourse.bass as bass

ROUNDS = 6
COLS = 64
RANKS = 4
ENGINES = 16

SCRATCH = {
    "slot0": ("sbuf", [128, RANKS * COLS], "bfloat16"),
    "slot1": ("sbuf", [128, RANKS * COLS], "bfloat16"),
}
SEMAPHORES = ["loaded", "stored", "left", "arrived0", "arrived1"]


def rank_program(g, core, T, topo):
    rank = T.rank_of(core)
    if rank is None:
        return
    slots = [T.slot0, T.slot1]
    arrived = [T.sem.arrived0, T.sem.arrived1]
    peers = [c for c in T.cores if c != core]
    peer_ids = []
    for c in peers:
        rid, pid, ring = topo.addr(c)
        peer_ids.append(bass.DstId(rid=rid, pnc=pid))
    lo, hi = rank * COLS, (rank + 1) * COLS

    def load(k):
        g.dma_start(slots[k % 2][:, lo:hi], T.x[k]).then_inc(T.sem.loaded, 16)

    load(0)
    for k in range(ROUNDS):
        s = k % 2
        own = slots[s][:, lo:hi]
        g.wait_ge(T.sem.loaded, 16 * (k + 1))
        g.remote_dma_fused(
            [bass.RemoteDMATransfer(
                dst_ids=peer_ids,
                dma_engine_mask=0xFFFF,
                remote_sem=arrived[s],
                srcs=[own],
                dsts=[own for c in peers],
            )],
            local_sem=T.sem.left,
        )
        if k + 1 < ROUNDS:
            load(k + 1)
        g.wait_ge(arrived[s], len(peers) * ENGINES * (k // 2 + 1))
        g.dma_start(T.y[k], slots[s][:]).then_inc(T.sem.stored, 16)
        g.wait_ge(T.sem.left, ENGINES * (k + 1))
        g.wait_ge(T.sem.stored, 16 * (k + 1))
